import numpy as np
import ml_dtypes


def mxq(x, axis, fmt="e4m3"):
    dtype, down = {"e4m3": (ml_dtypes.float8_e4m3fn, 7), "e5m2": (ml_dtypes.float8_e5m2, 14)}[fmt]
    v = np.moveaxis(np.asarray(x, np.float32).astype(ml_dtypes.bfloat16).astype(np.float64), axis, -1)
    blocks = v.reshape(v.shape[:-1] + (-1, 32))
    amax = np.abs(blocks).max(-1, keepdims=True)
    byte = np.maximum(np.where(amax > 0, np.frexp(amax)[1] - 1 + 127, 0) - down, 1)
    scale = np.exp2(byte - 127.0)
    codes = (blocks / scale).astype(np.float32).astype(dtype).astype(np.float64)
    return np.moveaxis((codes * scale).reshape(v.shape), -1, axis)


WIDE = False


def mx_kscale(k):
    if not WIDE:
        return np.ones(k)
    levels = np.array([30, -30])
    if k % 512:
        return np.exp2(np.random.permutation(np.resize(levels, k // 32))).repeat(32)
    a = np.empty((k // 512, 16))
    for p in range(k // 512):
        a[p, :8] = np.random.permutation(np.resize(levels, 8))
        for g in range(8):
            far = levels[np.abs(levels - a[p, g]) >= 10]
            a[p, g + 8] = far[np.random.randint(len(far))]
    return np.exp2(a.ravel()).repeat(32)


def f64(x):
    return np.asarray(x).astype(np.float64)


def striped(idx):
    return np.tile(np.asarray(idx).reshape(-1, 16).T, (8, 1)).astype(np.uint16)


def unstriped(offs):
    return offs[:16].T.reshape(-1).astype(np.int64)


E2M1 = np.array([0.0, 0.5, 1.0, 1.5, 2.0, 3.0, 4.0, 6.0, -0.0, -0.5, -1.0, -1.5, -2.0, -3.0, -4.0, -6.0])


def pack_weight(w, fmt):
    k, n = w.shape
    w = f64(np.asarray(w, np.float32).astype(ml_dtypes.bfloat16)).reshape(k // 32, 32, n)
    amax = np.abs(w).max(1)
    if fmt == "e4m3":
        byte = np.frexp(amax)[1] - 1 + 127 - 7
    else:
        mant, ex = np.frexp(amax / 6.0)
        byte = np.where(mant > 0.5, ex, ex - 1) + 127
    byte = np.clip(np.where(amax > 0, byte, 1), 1, 254)
    scaled = (w * np.exp2(127.0 - byte)[:, None, :]).reshape(k, n).astype(np.float32)
    by_word = np.ascontiguousarray(scaled.reshape(k // 512, 128, 4, n).transpose(0, 1, 3, 2))
    if fmt == "e4m3":
        words = by_word.astype(ml_dtypes.float8_e4m3fn).view(np.uint8)
    else:
        c = by_word.astype(ml_dtypes.float4_e2m1fn).view(np.uint8) & 0xF
        words = (c[..., 0::2] | (c[..., 1::2] << 4)).reshape(k // 512, 128, 2 * n)
    return np.ascontiguousarray(words), np.ascontiguousarray(byte.astype(np.uint8).reshape(k // 512, 16, n))


def unpack_weight(words, scales, fmt):
    g, _, n = scales.shape
    words = np.ascontiguousarray(words).reshape(g, 128, n, -1)
    if fmt == "e4m3":
        vals = words.view(ml_dtypes.float8_e4m3fn).astype(np.float64)
    else:
        nib = np.empty((g, 128, n, 4), np.uint8)
        nib[..., 0::2] = words & 0xF
        nib[..., 1::2] = words >> 4
        vals = E2M1[nib]
    vals = vals * np.repeat(np.exp2(scales.astype(np.float64) - 127.0), 8, axis=1)[..., None]
    return vals.transpose(0, 1, 3, 2).reshape(g * 512, n)


K, T, C, J, N = 512, 512, 2048, 512, 512


def setup_inputs():
    n = np.random.standard_normal
    idx = np.random.permutation(C)[:J]
    fk = mx_kscale(K)
    fj = mx_kscale(J)
    tq = np.exp(2 * n((T, J)))
    xtp = pack_weight(n((K, T)) * 0.3 / fk[:, None], "e4m3")
    wcp = pack_weight(n((K, C)) * 1 / np.sqrt(K) * fk[:, None], "e2m1")
    wop = pack_weight(n((J, N)) * 1 / np.sqrt(J) / fj[:, None], "e4m3")
    return {
        "xt_words": xtp[0],
        "xt_scales": xtp[1],
        "wc_words": wcp[0],
        "wc_scales": wcp[1],
        "tg": (tq / tq.sum(axis=1, keepdims=True)).astype(np.float32),
        "fj": (np.random.uniform(16.0, 32.0, (J, 1)) * fj[:, None]).astype(np.float32),
        "wo_words": wop[0],
        "wo_scales": wop[1],
        "offs": striped(idx),
    }


def reference(xt_words, xt_scales, wc_words, wc_scales, tg, fj, wo_words, wo_scales, offs):
    idx = unstriped(offs)
    xtu = unpack_weight(xt_words, xt_scales, "e4m3")
    wcu = unpack_weight(wc_words, wc_scales, "e2m1")
    wou = unpack_weight(wo_words, wo_scales, "e4m3")
    wcidxg = wcu[:, idx]
    z = xtu.T @ wcidxg
    p = np.exp(z)
    d = p / np.sum(p, axis=1, keepdims=True) - f64(tg)
    dt = d.T
    dw = dt * f64(fj)
    dwq = mxq(dw, 0, "e5m2")
    y = wou.T @ dwq
    return y

@@ -1,0 +1,135 @@
+from contextlib import ExitStack
+
+import concourse.mybir as mybir
+
+K, T, C, J, N = 512, 512, 2048, 512, 512
+FLOPS = 2 * K * T * J + 2 * J * N * T
+
+F32 = mybir.dt.float32
+BF16 = mybir.dt.bfloat16
+I32 = mybir.dt.int32
+U32 = mybir.dt.uint32
+U16 = mybir.dt.uint16
+U8 = mybir.dt.uint8
+E4M3 = mybir.dt.float8_e4m3fn_x4
+E5M2 = mybir.dt.float8_e5m2_x4
+E2M1 = mybir.dt.float4_e2m1fn_x4
+ACT = mybir.ActivationFunctionType
+ALU = mybir.AluOpType
+AX = mybir.AxisListType
+
+P = 128
+PACK = 4
+BLOCKS = T // P
+
+
+def load_scale_rows(queues, plane, rows):
+    for quad, queue in enumerate(queues):
+        queue.dma_start(out=plane[32 * quad : 32 * quad + 4, :].bitcast(I32), in_=rows[0, 4 * quad : 4 * quad + 4, :].bitcast(I32))
+
+
+def tile_list_class_error_back_kernel(tc, xt_words, xt_scales, wc_words, wc_scales, tg, fj, wo_words, wo_scales, offs, out):
+    nc = tc.nc
+    with ExitStack() as ctx:
+        keep = ctx.enter_context(tc.tile_pool(name="keep", bufs=1))
+        psum = ctx.enter_context(tc.psum_pool(name="psum", bufs=1))
+
+        offsets = keep.tile([P, J // 16], U16, name="offsets")
+        nc.sync.dma_start(offsets[:], offs)
+
+        ones = keep.tile([P, P], F32, name="ones", tag="tg_first")
+        nc.vector.memset(ones[:], 1.0)
+        wc_plane = keep.tile([P, C], U8, name="wc_plane", tag="wc_plane", align_bytes=64)
+        nc.vector.memset(wc_plane[:, : C // 2].bitcast(I32), 0)
+        nc.gpsimd.memset(wc_plane[:, C // 2 :].bitcast(I32), 0)
+        load_scale_rows([nc.sync] * 4, wc_plane, wc_scales)
+
+        wc_table = keep.tile([P, C], U16, name="wc_table", align_bytes=64)
+        nc.scalar.dma_start(out=wc_table[:].bitcast(I32), in_=wc_words[0].bitcast(I32))
+        fixed_words = keep.tile([P, T], U32, name="fixed_words", align_bytes=64)
+        nc.scalar.dma_start(out=fixed_words[:].bitcast(I32), in_=xt_words[0].rearrange("p n t -> p (n t)").bitcast(I32))
+
+        ident = keep.tile([P, P], F32, name="ident")
+        nc.gpsimd.affine_select(out=ident[:], in_=ones[:], compare_op=ALU.is_equal, fill=0.0, base=0, pattern=[[-1, P]], channel_multiplier=1)
+
+        tg_rows = tg.rearrange("(h b p) j -> h p b j", h=2, p=P)
+        tg_first = keep.tile([P, 2, J], F32, name="tg_first", tag="tg_first")
+        nc.sync.dma_start(out=tg_first[:], in_=tg_rows[0])
+
+        fixed_plane = keep.tile([P, T], U8, name="fixed_plane", align_bytes=64)
+        nc.gpsimd.memset(fixed_plane[:].bitcast(I32), 0)
+        load_scale_rows([nc.sync, nc.sync, nc.gpsimd, nc.gpsimd], fixed_plane, xt_scales)
+
+        warm = keep.tile([P, 1], F32, name="warm", tag="tg_second")
+        nc.scalar.activation(out=warm[:], in_=ident[:, 0:1], func=ACT.Exp)
+        tg_second = keep.tile([P, 2, J], F32, name="tg_second", tag="tg_second")
+        nc.sync.dma_start(out=tg_second[:], in_=tg_rows[1])
+
+        picked_words = keep.tile([P, J], U16, name="picked_words", align_bytes=64)
+        nc.vector.tensor_copy(picked_words[:], wc_table[:].indirect(offsets[:]))
+        picked_plane = keep.tile([P, J], U8, name="picked_plane", align_bytes=64)
+        nc.vector.tensor_copy(picked_plane[:], wc_plane[:].indirect(offsets[:]))
+
+        factors = keep.tile([P, PACK], F32, name="factors", tag="wc_plane", align_bytes=64)
+        nc.sync.dma_start(out=factors[:], in_=fj.rearrange("(p r) o -> p (r o)", r=PACK))
+
+        turned = [psum.tile([P, PACK, P], F32, name="turned%d" % b) for b in range(BLOCKS)]
+        minus_tg = [keep.tile([P, PACK, P], F32, name="minus_tg%d" % b) for b in range(BLOCKS)]
+        for b in range(BLOCKS):
+            src = (tg_first, tg_second)[b // 2][:, b % 2, :]
+            if b < BLOCKS - 1:
+                nc.scalar.activation(out=minus_tg[b][:].rearrange("p r q -> p q r"), in_=src.rearrange("p (q r) -> p q r", r=PACK), func=ACT.Copy, scale=-1.0)
+            else:
+                nc.gpsimd.tensor_scalar(out=minus_tg[b][:].rearrange("p r (g q) -> p g r q", q=PACK), in0=src.rearrange("p (g q r) -> p g r q", q=PACK, r=PACK), scalar1=-1.0, scalar2=1.0, op0=ALU.mult, op1=ALU.mult)
+
+        def turn(b, src, first):
+            for r in range(PACK):
+                nc.tensor.matmul(turned[b][:, r, :], src[:, r, :], ident[:], start=first and r == 0, stop=(not first) and r == PACK - 1, is_transpose=True)
+
+        logits = [psum.tile([P, J], F32, name="logits%d" % b, tag="bank%d" % b) for b in range(BLOCKS)]
+        for b in range(BLOCKS):
+            cols = slice(b * P, (b + 1) * P)
+            nc.tensor.matmul_mx(out=logits[b][:], lhsT=fixed_words[:, cols].bitcast(E4M3), lhsT_scale=fixed_plane[:, cols],
+                                rhs=picked_words[:].bitcast(E2M1), rhs_scale=picked_plane[:], start=True, stop=True)
+        for b in range(BLOCKS):
+            turn(b, minus_tg[b], True)
+
+        nc.sync.dma_start(out=fixed_words[:].bitcast(I32), in_=wo_words[0].rearrange("p n t -> p (n t)").bitcast(I32))
+        load_scale_rows([nc.sync] * 4, fixed_plane, wo_scales)
+
+        codes = keep.tile([P, T], U32, name="codes", align_bytes=64)
+        plane = keep.tile([P, T], U8, name="plane", align_bytes=64)
+        stats = [keep.tile([P, 24], F32, name="stats%d" % b) for b in range(BLOCKS)]
+        shares = [keep.tile([P, PACK, P], F32, name="shares%d" % b) for b in range(BLOCKS)]
+        for b in range(BLOCKS):
+            minus_max, total = stats[b][:, 0:1], stats[b][:, 8:9]
+            nc.vector.tensor_reduce(out=minus_max, in_=logits[b][:], axis=AX.X, op=ALU.max, negate=True)
+            nc.scalar.activation(out=shares[b][:], in_=logits[b][:].rearrange("p (q r) -> p r q", r=PACK), func=ACT.Exp, bias=minus_max, accum_out=total)
+            nc.vector.reciprocal(out=stats[b][:, 16:17], in_=total)
+        for b in range(BLOCKS):
+            inverse = stats[b][:, 16:17]
+            normed = keep.tile([P, PACK, P], F32, name="normed%d" % b)
+            if b < BLOCKS - 1:
+                nc.gpsimd.tensor_scalar(out=normed[:], in0=shares[b][:], scalar1=inverse, scalar2=1.0, op0=ALU.mult, op1=ALU.mult)
+            else:
+                nc.scalar.activation(out=normed[:], in_=shares[b][:], func=ACT.Copy, scale=inverse)
+            turn(b, normed, False)
+        errors = [keep.tile([P, P, PACK], BF16, name="errors%d" % b, align_bytes=64) for b in range(BLOCKS)]
+        for b in range(BLOCKS):
+            nc.vector.tensor_tensor(out=errors[b][:], in0=turned[b][:].rearrange("p r t -> p t r"),
+                                    in1=factors[:].unsqueeze(1).to_broadcast([P, P, PACK]), op=ALU.mult)
+        for b in range(BLOCKS):
+            cols = slice(b * P, (b + 1) * P)
+            nc.vector.quantize_mx(out=codes[:, cols].bitcast(E5M2), scales=plane[:, cols], in_=errors[b][:].rearrange("p t r -> p (t r)"))
+
+        for b in range(N // P):
+            cols = slice(b * P, (b + 1) * P)
+            acc = psum.tile([P, T], F32, name="acc%d" % b, tag="bank%d" % b)
+            nc.tensor.matmul_mx(out=acc[:], lhsT=fixed_words[:, cols].bitcast(E4M3), lhsT_scale=fixed_plane[:, cols],
+                                rhs=codes[:].bitcast(E5M2), rhs_scale=plane[:], start=True, stop=True)
+            result = keep.tile([P, T], F32, name="result%d" % b)
+            if b % 2 == 0:
+                nc.scalar.copy(out=result[:], in_=acc[:])
+            else:
+                nc.vector.tensor_copy(out=result[:], in_=acc[:])
+            nc.sync.dma_start(out=out[cols, :], in_=result[:])

@@ -32,85 +32,87 @@ def tile_list_class_error_back_kernel(tc, xt_words, xt_scales, wc_words, wc_scal
     nc = tc.nc
     with ExitStack() as ctx:
         keep = ctx.enter_context(tc.tile_pool(name="keep", bufs=1))
+        late = ctx.enter_context(tc.tile_pool(name="late", bufs=1))
         psum = ctx.enter_context(tc.psum_pool(name="psum", bufs=1))
 
         offsets = keep.tile([P, J // 16], U16, name="offsets")
         nc.sync.dma_start(offsets[:], offs)
 
-        ones = keep.tile([P, P], F32, name="ones", tag="tg_first")
-        nc.vector.memset(ones[:], 1.0)
         wc_plane = keep.tile([P, C], U8, name="wc_plane", tag="wc_plane", align_bytes=64)
-        nc.vector.memset(wc_plane[:, : C // 2].bitcast(I32), 0)
-        nc.gpsimd.memset(wc_plane[:, C // 2 :].bitcast(I32), 0)
+        nc.vector.memset(wc_plane[:].bitcast(I32), 0)
         load_scale_rows([nc.sync] * 4, wc_plane, wc_scales)
-
         wc_table = keep.tile([P, C], U16, name="wc_table", align_bytes=64)
-        nc.scalar.dma_start(out=wc_table[:].bitcast(I32), in_=wc_words[0].bitcast(I32))
+        nc.sync.dma_start(out=wc_table[:].bitcast(I32), in_=wc_words[0].bitcast(I32))
         fixed_words = keep.tile([P, T], U32, name="fixed_words", align_bytes=64)
-        nc.scalar.dma_start(out=fixed_words[:].bitcast(I32), in_=xt_words[0].rearrange("p n t -> p (n t)").bitcast(I32))
+        nc.sync.dma_start(out=fixed_words[:].bitcast(I32), in_=xt_words[0].rearrange("p n t -> p (n t)").bitcast(I32))
+        fixed_plane = keep.tile([P, T], U8, name="fixed_plane", align_bytes=64)
+        nc.vector.memset(fixed_plane[:].bitcast(I32), 0)
+        load_scale_rows([nc.sync] * 4, fixed_plane, xt_scales)
 
+        ones = keep.tile([P, P], F32, name="ones")
+        nc.gpsimd.memset(ones[:], 1.0)
         ident = keep.tile([P, P], F32, name="ident")
         nc.gpsimd.affine_select(out=ident[:], in_=ones[:], compare_op=ALU.is_equal, fill=0.0, base=0, pattern=[[-1, P]], channel_multiplier=1)
 
-        tg_rows = tg.rearrange("(h b p) j -> h p b j", h=2, p=P)
-        tg_first = keep.tile([P, 2, J], F32, name="tg_first", tag="tg_first")
-        nc.sync.dma_start(out=tg_first[:], in_=tg_rows[0])
+        half = 2 * J * 4
+        warm = keep.tile([P, 16], F32, name="warm")
+        nc.scalar.activation(out=warm[:], in_=ones[:, 0:16], func=ACT.Exp)
+        targets = [late.tile([P, 2, J], F32, name="targets%d" % h, offset=h * half) for h in range(2)]
+        for b in range(BLOCKS):
+            nc.sync.dma_start(out=targets[b // 2][:, b % 2, :], in_=tg[b * P : (b + 1) * P, :])
 
-        fixed_plane = keep.tile([P, T], U8, name="fixed_plane", align_bytes=64)
-        nc.gpsimd.memset(fixed_plane[:].bitcast(I32), 0)
-        load_scale_rows([nc.sync, nc.sync, nc.gpsimd, nc.gpsimd], fixed_plane, xt_scales)
-
-        warm = keep.tile([P, 1], F32, name="warm", tag="tg_second")
-        nc.scalar.activation(out=warm[:], in_=ident[:, 0:1], func=ACT.Exp)
-        tg_second = keep.tile([P, 2, J], F32, name="tg_second", tag="tg_second")
-        nc.sync.dma_start(out=tg_second[:], in_=tg_rows[1])
-
-        picked_words = keep.tile([P, J], U16, name="picked_words", align_bytes=64)
-        nc.vector.tensor_copy(picked_words[:], wc_table[:].indirect(offsets[:]))
         picked_plane = keep.tile([P, J], U8, name="picked_plane", align_bytes=64)
+        picked_words = keep.tile([P, J], U16, name="picked_words", align_bytes=64)
+        halves = [slice(h * J // 2, (h + 1) * J // 2) for h in range(2)]
         nc.vector.tensor_copy(picked_plane[:], wc_plane[:].indirect(offsets[:]))
+        for h in range(2):
+            nc.vector.tensor_copy(picked_words[:, halves[h]], wc_table[:].indirect(offsets[:, h * J // 32 : (h + 1) * J // 32]))
 
         factors = keep.tile([P, PACK], F32, name="factors", tag="wc_plane", align_bytes=64)
-        nc.sync.dma_start(out=factors[:], in_=fj.rearrange("(p r) o -> p (r o)", r=PACK))
+        nc.gpsimd.dma_start(out=factors[:], in_=fj.rearrange("(p r) o -> p (r o)", r=PACK))
+
+        logits = [psum.tile([P, J], F32, name="logits%d" % b, tag="bank%d" % b) for b in range(BLOCKS)]
+        stats = [keep.tile([P, 24], F32, name="stats%d" % b) for b in range(BLOCKS)]
+        for b, classes in [(0, halves[0]), (1, halves[0]), (0, halves[1]), (1, halves[1]), (2, slice(0, J)), (3, slice(0, J))]:
+            cols = slice(b * P, (b + 1) * P)
+            nc.tensor.matmul_mx(out=logits[b][:, classes], lhsT=fixed_words[:, cols].bitcast(E4M3), lhsT_scale=fixed_plane[:, cols],
+                                rhs=picked_words[:, classes].bitcast(E2M1), rhs_scale=picked_plane[:, classes], start=True, stop=True)
+
+        nc.sync.dma_start(out=fixed_words[:].bitcast(I32), in_=wo_words[0].rearrange("p n t -> p (n t)").bitcast(I32))
+        load_scale_rows([nc.sync] * 4, fixed_plane, wo_scales)
 
         turned = [psum.tile([P, PACK, P], F32, name="turned%d" % b) for b in range(BLOCKS)]
-        minus_tg = [keep.tile([P, PACK, P], F32, name="minus_tg%d" % b) for b in range(BLOCKS)]
-        for b in range(BLOCKS):
-            src = (tg_first, tg_second)[b // 2][:, b % 2, :]
-            if b < BLOCKS - 1:
-                nc.scalar.activation(out=minus_tg[b][:].rearrange("p r q -> p q r"), in_=src.rearrange("p (q r) -> p q r", r=PACK), func=ACT.Copy, scale=-1.0)
-            else:
-                nc.gpsimd.tensor_scalar(out=minus_tg[b][:].rearrange("p r (g q) -> p g r q", q=PACK), in0=src.rearrange("p (g q r) -> p g r q", q=PACK, r=PACK), scalar1=-1.0, scalar2=1.0, op0=ALU.mult, op1=ALU.mult)
 
         def turn(b, src, first):
             for r in range(PACK):
                 nc.tensor.matmul(turned[b][:, r, :], src[:, r, :], ident[:], start=first and r == 0, stop=(not first) and r == PACK - 1, is_transpose=True)
 
-        logits = [psum.tile([P, J], F32, name="logits%d" % b, tag="bank%d" % b) for b in range(BLOCKS)]
-        for b in range(BLOCKS):
-            cols = slice(b * P, (b + 1) * P)
-            nc.tensor.matmul_mx(out=logits[b][:], lhsT=fixed_words[:, cols].bitcast(E4M3), lhsT_scale=fixed_plane[:, cols],
-                                rhs=picked_words[:].bitcast(E2M1), rhs_scale=picked_plane[:], start=True, stop=True)
-        for b in range(BLOCKS):
-            turn(b, minus_tg[b], True)
+        def negate_targets(b):
+            src = targets[b // 2][:, b % 2, :]
+            minus_tg = keep.tile([P, PACK, P], F32, name="minus_tg%d" % b)
+            if b >= 2:
+                nc.gpsimd.tensor_scalar(out=minus_tg[:].rearrange("p r (g q) -> p g r q", q=PACK), in0=src.rearrange("p (g q r) -> p g r q", q=PACK, r=PACK), scalar1=-1.0, scalar2=1.0, op0=ALU.mult, op1=ALU.mult)
+            else:
+                nc.scalar.activation(out=minus_tg[:].rearrange("p r q -> p q r"), in_=src.rearrange("p (q r) -> p q r", r=PACK), func=ACT.Copy, scale=-1.0)
+            turn(b, minus_tg, True)
 
-        nc.sync.dma_start(out=fixed_words[:].bitcast(I32), in_=wo_words[0].rearrange("p n t -> p (n t)").bitcast(I32))
-        load_scale_rows([nc.sync] * 4, fixed_plane, wo_scales)
+        for b in range(BLOCKS):
+            negate_targets(b)
 
         codes = keep.tile([P, T], U32, name="codes", align_bytes=64)
         plane = keep.tile([P, T], U8, name="plane", align_bytes=64)
-        stats = [keep.tile([P, 24], F32, name="stats%d" % b) for b in range(BLOCKS)]
-        shares = [keep.tile([P, PACK, P], F32, name="shares%d" % b) for b in range(BLOCKS)]
+        shares = [late.tile([P, PACK, P], F32, name="shares0", offset=0)]
+        shares.extend(keep.tile([P, PACK, P], F32, name="shares%d" % b, tag="shares%d" % b) for b in range(1, BLOCKS))
         for b in range(BLOCKS):
             minus_max, total = stats[b][:, 0:1], stats[b][:, 8:9]
             nc.vector.tensor_reduce(out=minus_max, in_=logits[b][:], axis=AX.X, op=ALU.max, negate=True)
             nc.scalar.activation(out=shares[b][:], in_=logits[b][:].rearrange("p (q r) -> p r q", r=PACK), func=ACT.Exp, bias=minus_max, accum_out=total)
-            nc.vector.reciprocal(out=stats[b][:, 16:17], in_=total)
         for b in range(BLOCKS):
-            inverse = stats[b][:, 16:17]
+            total, inverse = stats[b][:, 8:9], stats[b][:, 16:17]
+            nc.vector.reciprocal(out=inverse, in_=total)
             normed = keep.tile([P, PACK, P], F32, name="normed%d" % b)
-            if b < BLOCKS - 1:
-                nc.gpsimd.tensor_scalar(out=normed[:], in0=shares[b][:], scalar1=inverse, scalar2=1.0, op0=ALU.mult, op1=ALU.mult)
+            if b < 2:
+                nc.vector.tensor_scalar(out=normed[:], in0=shares[b][:], scalar1=inverse, scalar2=None, op0=ALU.mult)
             else:
                 nc.scalar.activation(out=normed[:], in_=shares[b][:], func=ACT.Copy, scale=inverse)
             turn(b, normed, False)

@@ -38,9 +38,13 @@ def tile_list_class_error_back_kernel(tc, xt_words, xt_scales, wc_words, wc_scal
         offsets = keep.tile([P, J // 16], U16, name="offsets")
         nc.sync.dma_start(offsets[:], offs)
 
-        wc_plane = keep.tile([P, C], U8, name="wc_plane", tag="wc_plane", align_bytes=64)
-        nc.vector.memset(wc_plane[:].bitcast(I32), 0)
-        load_scale_rows([nc.sync] * 4, wc_plane, wc_scales)
+        factors = keep.tile([P, PACK], F32, name="factors")
+        nc.sync.dma_start(out=factors[:], in_=fj.rearrange("(p r) o -> p (r o)", r=PACK))
+
+        wc_plane = keep.tile([P, C], U8, name="wc_plane", align_bytes=64)
+        nc.vector.memset(wc_plane[:, : C // 2].bitcast(I32), 0)
+        nc.gpsimd.memset(wc_plane[:, C // 2 :].bitcast(I32), 0)
+        load_scale_rows([nc.sync, nc.scalar] * 2, wc_plane, wc_scales)
         wc_table = keep.tile([P, C], U16, name="wc_table", align_bytes=64)
         nc.sync.dma_start(out=wc_table[:].bitcast(I32), in_=wc_words[0].bitcast(I32))
         fixed_words = keep.tile([P, T], U32, name="fixed_words", align_bytes=64)
@@ -56,7 +60,7 @@ def tile_list_class_error_back_kernel(tc, xt_words, xt_scales, wc_words, wc_scal
 
         half = 2 * J * 4
         warm = keep.tile([P, 16], F32, name="warm")
-        nc.scalar.activation(out=warm[:], in_=ones[:, 0:16], func=ACT.Exp)
+        nc.scalar.activation(out=warm[:], in_=ident[:, 0:16], func=ACT.Exp)
         targets = [late.tile([P, 2, J], F32, name="targets%d" % h, offset=h * half) for h in range(2)]
         for b in range(BLOCKS):
             nc.sync.dma_start(out=targets[b // 2][:, b % 2, :], in_=tg[b * P : (b + 1) * P, :])
@@ -67,9 +71,6 @@ def tile_list_class_error_back_kernel(tc, xt_words, xt_scales, wc_words, wc_scal
         nc.vector.tensor_copy(picked_plane[:], wc_plane[:].indirect(offsets[:]))
         for h in range(2):
             nc.vector.tensor_copy(picked_words[:, halves[h]], wc_table[:].indirect(offsets[:, h * J // 32 : (h + 1) * J // 32]))
-
-        factors = keep.tile([P, PACK], F32, name="factors", tag="wc_plane", align_bytes=64)
-        nc.gpsimd.dma_start(out=factors[:], in_=fj.rearrange("(p r) o -> p (r o)", r=PACK))
 
         logits = [psum.tile([P, J], F32, name="logits%d" % b, tag="bank%d" % b) for b in range(BLOCKS)]
         stats = [keep.tile([P, 24], F32, name="stats%d" % b) for b in range(BLOCKS)]
@@ -99,39 +100,69 @@ def tile_list_class_error_back_kernel(tc, xt_words, xt_scales, wc_words, wc_scal
         for b in range(BLOCKS):
             negate_targets(b)
 
-        codes = keep.tile([P, T], U32, name="codes", align_bytes=64)
-        plane = keep.tile([P, T], U8, name="plane", align_bytes=64)
+        pad = T // 2
+        codes = keep.tile([P, pad + T], U32, name="codes", align_bytes=64)
+        plane = keep.tile([P, pad + T], U8, name="plane", align_bytes=64)
+        nc.gpsimd.memset(codes[:, :pad].bitcast(I32), 0)
+        nc.gpsimd.memset(plane[:, :pad].bitcast(I32), 0)
         shares = [late.tile([P, PACK, P], F32, name="shares0", offset=0)]
         shares.extend(keep.tile([P, PACK, P], F32, name="shares%d" % b, tag="shares%d" % b) for b in range(1, BLOCKS))
-        for b in range(BLOCKS):
+
+        def exponentiate(b):
             minus_max, total = stats[b][:, 0:1], stats[b][:, 8:9]
             nc.vector.tensor_reduce(out=minus_max, in_=logits[b][:], axis=AX.X, op=ALU.max, negate=True)
             nc.scalar.activation(out=shares[b][:], in_=logits[b][:].rearrange("p (q r) -> p r q", r=PACK), func=ACT.Exp, bias=minus_max, accum_out=total)
-        for b in range(BLOCKS):
+
+        def normalise(b):
             total, inverse = stats[b][:, 8:9], stats[b][:, 16:17]
             nc.vector.reciprocal(out=inverse, in_=total)
             normed = keep.tile([P, PACK, P], F32, name="normed%d" % b)
-            if b < 2:
-                nc.vector.tensor_scalar(out=normed[:], in0=shares[b][:], scalar1=inverse, scalar2=None, op0=ALU.mult)
-            else:
+            if b == 2:
                 nc.scalar.activation(out=normed[:], in_=shares[b][:], func=ACT.Copy, scale=inverse)
+            else:
+                nc.vector.tensor_scalar(out=normed[:], in0=shares[b][:], scalar1=inverse, scalar2=None, op0=ALU.mult)
             turn(b, normed, False)
+
         errors = [keep.tile([P, P, PACK], BF16, name="errors%d" % b, align_bytes=64) for b in range(BLOCKS)]
-        for b in range(BLOCKS):
+
+        def weigh(b):
             nc.vector.tensor_tensor(out=errors[b][:], in0=turned[b][:].rearrange("p r t -> p t r"),
                                     in1=factors[:].unsqueeze(1).to_broadcast([P, P, PACK]), op=ALU.mult)
-        for b in range(BLOCKS):
-            cols = slice(b * P, (b + 1) * P)
+
+        def quantise(b):
+            cols = slice(pad + b * P, pad + (b + 1) * P)
             nc.vector.quantize_mx(out=codes[:, cols].bitcast(E5M2), scales=plane[:, cols], in_=errors[b][:].rearrange("p t r -> p (t r)"))
 
-        for b in range(N // P):
-            cols = slice(b * P, (b + 1) * P)
-            acc = psum.tile([P, T], F32, name="acc%d" % b, tag="bank%d" % b)
-            nc.tensor.matmul_mx(out=acc[:], lhsT=fixed_words[:, cols].bitcast(E4M3), lhsT_scale=fixed_plane[:, cols],
-                                rhs=codes[:].bitcast(E5M2), rhs_scale=plane[:], start=True, stop=True)
-            result = keep.tile([P, T], F32, name="result%d" % b)
-            if b % 2 == 0:
-                nc.scalar.copy(out=result[:], in_=acc[:])
-            else:
-                nc.vector.tensor_copy(out=result[:], in_=acc[:])
-            nc.sync.dma_start(out=out[cols, :], in_=result[:])
+        def product(b, first_column, skip, bank, copy):
+            rows = slice(b * P, (b + 1) * P)
+            window = slice(first_column, first_column + T)
+            acc = psum.tile([P, T], F32, name="acc", tag=bank)
+            nc.tensor.matmul_mx(out=acc[:], lhsT=fixed_words[:, rows].bitcast(E4M3), lhsT_scale=fixed_plane[:, rows],
+                                rhs=codes[:, window].bitcast(E5M2), rhs_scale=plane[:, window], start=True, stop=True)
+            result = keep.tile([P, T - skip], F32, name="result", tag="result_" + bank)
+            copy(out=result[:], in_=acc[:, skip:])
+            first_token = first_column + skip - pad
+            nc.sync.dma_start(out=out[rows, first_token : first_token + T - skip], in_=result[:])
+
+        exponentiate(0)
+        exponentiate(1)
+        normalise(0)
+        exponentiate(2)
+        normalise(1)
+        exponentiate(3)
+        weigh(0)
+        normalise(2)
+        normalise(3)
+        weigh(1)
+        quantise(0)
+        weigh(2)
+        quantise(1)
+        weigh(3)
+        product(0, 0, pad, "bank0", nc.scalar.copy)
+        product(1, 0, pad, "bank1", nc.scalar.copy)
+        quantise(2)
+        quantise(3)
+        product(2, pad, 0, "bank2", nc.scalar.copy)
+        product(3, pad, 0, "bank3", nc.vector.tensor_copy)
+        product(0, pad, pad, "turned0", nc.scalar.copy)
+        product(1, pad, pad, "turned1", nc.vector.tensor_copy)

@@ -42,8 +42,7 @@ def tile_list_class_error_back_kernel(tc, xt_words, xt_scales, wc_words, wc_scal
         nc.sync.dma_start(out=factors[:], in_=fj.rearrange("(p r) o -> p (r o)", r=PACK))
 
         wc_plane = keep.tile([P, C], U8, name="wc_plane", align_bytes=64)
-        nc.vector.memset(wc_plane[:, : C // 2].bitcast(I32), 0)
-        nc.gpsimd.memset(wc_plane[:, C // 2 :].bitcast(I32), 0)
+        nc.vector.memset(wc_plane[:].bitcast(I32), 0)
         load_scale_rows([nc.sync, nc.scalar] * 2, wc_plane, wc_scales)
         wc_table = keep.tile([P, C], U16, name="wc_table", align_bytes=64)
         nc.sync.dma_start(out=wc_table[:].bitcast(I32), in_=wc_words[0].bitcast(I32))
@@ -54,7 +53,7 @@ def tile_list_class_error_back_kernel(tc, xt_words, xt_scales, wc_words, wc_scal
         load_scale_rows([nc.sync] * 4, fixed_plane, xt_scales)
 
         ones = keep.tile([P, P], F32, name="ones")
-        nc.gpsimd.memset(ones[:], 1.0)
+        nc.vector.memset(ones[:], 1.0)
         ident = keep.tile([P, P], F32, name="ident")
         nc.gpsimd.affine_select(out=ident[:], in_=ones[:], compare_op=ALU.is_equal, fill=0.0, base=0, pattern=[[-1, P]], channel_multiplier=1)
 
@@ -73,7 +72,6 @@ def tile_list_class_error_back_kernel(tc, xt_words, xt_scales, wc_words, wc_scal
             nc.vector.tensor_copy(picked_words[:, halves[h]], wc_table[:].indirect(offsets[:, h * J // 32 : (h + 1) * J // 32]))
 
         logits = [psum.tile([P, J], F32, name="logits%d" % b, tag="bank%d" % b) for b in range(BLOCKS)]
-        stats = [keep.tile([P, 24], F32, name="stats%d" % b) for b in range(BLOCKS)]
         for b, classes in [(0, halves[0]), (1, halves[0]), (0, halves[1]), (1, halves[1]), (2, slice(0, J)), (3, slice(0, J))]:
             cols = slice(b * P, (b + 1) * P)
             nc.tensor.matmul_mx(out=logits[b][:, classes], lhsT=fixed_words[:, cols].bitcast(E4M3), lhsT_scale=fixed_plane[:, cols],
@@ -91,8 +89,8 @@ def tile_list_class_error_back_kernel(tc, xt_words, xt_scales, wc_words, wc_scal
         def negate_targets(b):
             src = targets[b // 2][:, b % 2, :]
             minus_tg = keep.tile([P, PACK, P], F32, name="minus_tg%d" % b)
-            if b >= 2:
-                nc.gpsimd.tensor_scalar(out=minus_tg[:].rearrange("p r (g q) -> p g r q", q=PACK), in0=src.rearrange("p (g q r) -> p g r q", q=PACK, r=PACK), scalar1=-1.0, scalar2=1.0, op0=ALU.mult, op1=ALU.mult)
+            if b < 2:
+                nc.vector.tensor_scalar(out=minus_tg[:].rearrange("p r q -> p q r"), in0=src.rearrange("p (q r) -> p q r", r=PACK), scalar1=-1.0, scalar2=None, op0=ALU.mult)
             else:
                 nc.scalar.activation(out=minus_tg[:].rearrange("p r q -> p q r"), in_=src.rearrange("p (q r) -> p q r", r=PACK), func=ACT.Copy, scale=-1.0)
             turn(b, minus_tg, True)
@@ -103,9 +101,11 @@ def tile_list_class_error_back_kernel(tc, xt_words, xt_scales, wc_words, wc_scal
         pad = T // 2
         codes = keep.tile([P, pad + T], U32, name="codes", align_bytes=64)
         plane = keep.tile([P, pad + T], U8, name="plane", align_bytes=64)
-        nc.gpsimd.memset(codes[:, :pad].bitcast(I32), 0)
-        nc.gpsimd.memset(plane[:, :pad].bitcast(I32), 0)
-        shares = [late.tile([P, PACK, P], F32, name="shares0", offset=0)]
+        nc.vector.memset(codes[:, :pad].bitcast(I32), 0)
+        nc.vector.memset(plane[:, :pad].bitcast(I32), 0)
+        stats = [late.tile([P, 24], F32, name="stats0", offset=0)]
+        stats.extend(keep.tile([P, 24], F32, name="stats%d" % b) for b in range(1, BLOCKS))
+        shares = [late.tile([P, PACK, P], F32, name="shares0", offset=half)]
         shares.extend(keep.tile([P, PACK, P], F32, name="shares%d" % b, tag="shares%d" % b) for b in range(1, BLOCKS))
 
         def exponentiate(b):

@@ -20,47 +20,56 @@ AX = mybir.AxisListType
 
 P = 128
 PACK = 4
+QUADRANT = 32
+LIST_ROWS = 16
 BLOCKS = T // P
+PAD = T // 2
+PAIR_BYTES = 2 * J * 4
 
 
-def load_scale_rows(queues, plane, rows):
-    for quad, queue in enumerate(queues):
-        queue.dma_start(out=plane[32 * quad : 32 * quad + 4, :].bitcast(I32), in_=rows[0, 4 * quad : 4 * quad + 4, :].bitcast(I32))
+def load_plane(nc, plane, rows):
+    for quad in range(P // QUADRANT):
+        first = QUADRANT * quad
+        nc.sync.dma_start(out=plane[first : first + PACK, :].bitcast(I32), in_=rows[0, PACK * quad : PACK * (quad + 1), :].bitcast(I32))
+
+
+def load_words(nc, words, packed):
+    nc.sync.dma_start(out=words[:].bitcast(I32), in_=packed[0].rearrange("p n r -> p (n r)").bitcast(I32))
 
 
 def tile_list_class_error_back_kernel(tc, xt_words, xt_scales, wc_words, wc_scales, tg, fj, wo_words, wo_scales, offs, out):
     nc = tc.nc
     with ExitStack() as ctx:
         keep = ctx.enter_context(tc.tile_pool(name="keep", bufs=1))
-        late = ctx.enter_context(tc.tile_pool(name="late", bufs=1))
+        reused = ctx.enter_context(tc.tile_pool(name="reused", bufs=1))
         psum = ctx.enter_context(tc.psum_pool(name="psum", bufs=1))
 
-        offsets = keep.tile([P, J // 16], U16, name="offsets")
+        offsets = keep.tile([P, J // LIST_ROWS], U16, name="offsets")
         nc.sync.dma_start(offsets[:], offs)
-
         factors = keep.tile([P, PACK], F32, name="factors")
         nc.sync.dma_start(out=factors[:], in_=fj.rearrange("(p r) o -> p (r o)", r=PACK))
 
         wc_plane = keep.tile([P, C], U8, name="wc_plane", align_bytes=64)
         nc.vector.memset(wc_plane[:].bitcast(I32), 0)
-        load_scale_rows([nc.sync, nc.scalar] * 2, wc_plane, wc_scales)
+        load_plane(nc, wc_plane, wc_scales)
         wc_table = keep.tile([P, C], U16, name="wc_table", align_bytes=64)
         nc.sync.dma_start(out=wc_table[:].bitcast(I32), in_=wc_words[0].bitcast(I32))
+
         fixed_words = keep.tile([P, T], U32, name="fixed_words", align_bytes=64)
-        nc.sync.dma_start(out=fixed_words[:].bitcast(I32), in_=xt_words[0].rearrange("p n t -> p (n t)").bitcast(I32))
+        load_words(nc, fixed_words, xt_words)
         fixed_plane = keep.tile([P, T], U8, name="fixed_plane", align_bytes=64)
         nc.vector.memset(fixed_plane[:].bitcast(I32), 0)
-        load_scale_rows([nc.sync] * 4, fixed_plane, xt_scales)
+        load_plane(nc, fixed_plane, xt_scales)
 
         ones = keep.tile([P, P], F32, name="ones")
         nc.vector.memset(ones[:], 1.0)
         ident = keep.tile([P, P], F32, name="ident")
         nc.gpsimd.affine_select(out=ident[:], in_=ones[:], compare_op=ALU.is_equal, fill=0.0, base=0, pattern=[[-1, P]], channel_multiplier=1)
 
-        half = 2 * J * 4
         warm = keep.tile([P, 16], F32, name="warm")
-        nc.scalar.activation(out=warm[:], in_=ident[:, 0:16], func=ACT.Exp)
-        targets = [late.tile([P, 2, J], F32, name="targets%d" % h, offset=h * half) for h in range(2)]
+        nc.scalar.activation(out=warm[:], in_=ones[:, 0:16], func=ACT.Exp)
+
+        targets = [reused.tile([P, 2, J], F32, name="targets%d" % pair, offset=pair * PAIR_BYTES) for pair in range(BLOCKS // 2)]
         for b in range(BLOCKS):
             nc.sync.dma_start(out=targets[b // 2][:, b % 2, :], in_=tg[b * P : (b + 1) * P, :])
 
@@ -68,80 +77,77 @@ def tile_list_class_error_back_kernel(tc, xt_words, xt_scales, wc_words, wc_scal
         picked_words = keep.tile([P, J], U16, name="picked_words", align_bytes=64)
         halves = [slice(h * J // 2, (h + 1) * J // 2) for h in range(2)]
         nc.vector.tensor_copy(picked_plane[:], wc_plane[:].indirect(offsets[:]))
-        for h in range(2):
-            nc.vector.tensor_copy(picked_words[:, halves[h]], wc_table[:].indirect(offsets[:, h * J // 32 : (h + 1) * J // 32]))
+        for half in halves:
+            nc.vector.tensor_copy(picked_words[:, half], wc_table[:].indirect(offsets[:, half.start // LIST_ROWS : half.stop // LIST_ROWS]))
 
         logits = [psum.tile([P, J], F32, name="logits%d" % b, tag="bank%d" % b) for b in range(BLOCKS)]
-        for b, classes in [(0, halves[0]), (1, halves[0]), (0, halves[1]), (1, halves[1]), (2, slice(0, J)), (3, slice(0, J))]:
-            cols = slice(b * P, (b + 1) * P)
-            nc.tensor.matmul_mx(out=logits[b][:, classes], lhsT=fixed_words[:, cols].bitcast(E4M3), lhsT_scale=fixed_plane[:, cols],
+        passes = [(b, half) for half in halves for b in range(2)] + [(b, slice(0, J)) for b in range(2, BLOCKS)]
+        for b, classes in passes:
+            tokens = slice(b * P, (b + 1) * P)
+            nc.tensor.matmul_mx(out=logits[b][:, classes], lhsT=fixed_words[:, tokens].bitcast(E4M3), lhsT_scale=fixed_plane[:, tokens],
                                 rhs=picked_words[:, classes].bitcast(E2M1), rhs_scale=picked_plane[:, classes], start=True, stop=True)
 
-        nc.sync.dma_start(out=fixed_words[:].bitcast(I32), in_=wo_words[0].rearrange("p n t -> p (n t)").bitcast(I32))
-        load_scale_rows([nc.sync] * 4, fixed_plane, wo_scales)
+        load_words(nc, fixed_words, wo_words)
+        load_plane(nc, fixed_plane, wo_scales)
 
         turned = [psum.tile([P, PACK, P], F32, name="turned%d" % b) for b in range(BLOCKS)]
 
-        def turn(b, src, first):
+        def turn(b, src, opens):
             for r in range(PACK):
-                nc.tensor.matmul(turned[b][:, r, :], src[:, r, :], ident[:], start=first and r == 0, stop=(not first) and r == PACK - 1, is_transpose=True)
+                nc.tensor.matmul(turned[b][:, r, :], src[:, r, :], ident[:], start=opens and r == 0, stop=(not opens) and r == PACK - 1, is_transpose=True)
 
-        def negate_targets(b):
+        for b in range(BLOCKS):
             src = targets[b // 2][:, b % 2, :]
             minus_tg = keep.tile([P, PACK, P], F32, name="minus_tg%d" % b)
             if b < 2:
-                nc.vector.tensor_scalar(out=minus_tg[:].rearrange("p r q -> p q r"), in0=src.rearrange("p (q r) -> p q r", r=PACK), scalar1=-1.0, scalar2=None, op0=ALU.mult)
-            else:
                 nc.scalar.activation(out=minus_tg[:].rearrange("p r q -> p q r"), in_=src.rearrange("p (q r) -> p q r", r=PACK), func=ACT.Copy, scale=-1.0)
+            else:
+                nc.gpsimd.tensor_scalar(out=minus_tg[:].rearrange("p r (g q) -> p g r q", q=PACK), in0=src.rearrange("p (g q r) -> p g r q", q=PACK, r=PACK),
+                                        scalar1=-1.0, scalar2=1.0, op0=ALU.mult, op1=ALU.mult)
             turn(b, minus_tg, True)
 
-        for b in range(BLOCKS):
-            negate_targets(b)
+        codes = keep.tile([P, PAD + T], U32, name="codes", align_bytes=64)
+        plane = keep.tile([P, PAD + T], U8, name="plane", align_bytes=64)
+        nc.vector.memset(codes[:, :PAD].bitcast(I32), 0)
+        nc.vector.memset(plane[:, :PAD].bitcast(I32), 0)
 
-        pad = T // 2
-        codes = keep.tile([P, pad + T], U32, name="codes", align_bytes=64)
-        plane = keep.tile([P, pad + T], U8, name="plane", align_bytes=64)
-        nc.vector.memset(codes[:, :pad].bitcast(I32), 0)
-        nc.vector.memset(plane[:, :pad].bitcast(I32), 0)
-        stats = [late.tile([P, 24], F32, name="stats0", offset=0)]
-        stats.extend(keep.tile([P, 24], F32, name="stats%d" % b) for b in range(1, BLOCKS))
-        shares = [late.tile([P, PACK, P], F32, name="shares0", offset=half)]
-        shares.extend(keep.tile([P, PACK, P], F32, name="shares%d" % b, tag="shares%d" % b) for b in range(1, BLOCKS))
+        stats = [keep.tile([P, 3, 8], F32, name="stats%d" % b) for b in range(BLOCKS)]
+        powers = [reused.tile([P, PACK, P], F32, name="powers0", offset=0)]
+        powers.extend(keep.tile([P, PACK, P], F32, name="powers%d" % b) for b in range(1, BLOCKS))
+        errors = [keep.tile([P, P, PACK], BF16, name="errors%d" % b, align_bytes=64) for b in range(BLOCKS)]
 
         def exponentiate(b):
-            minus_max, total = stats[b][:, 0:1], stats[b][:, 8:9]
+            minus_max, total = stats[b][:, 0, 0:1], stats[b][:, 1, 0:1]
             nc.vector.tensor_reduce(out=minus_max, in_=logits[b][:], axis=AX.X, op=ALU.max, negate=True)
-            nc.scalar.activation(out=shares[b][:], in_=logits[b][:].rearrange("p (q r) -> p r q", r=PACK), func=ACT.Exp, bias=minus_max, accum_out=total)
+            nc.scalar.activation(out=powers[b][:], in_=logits[b][:].rearrange("p (q r) -> p r q", r=PACK), func=ACT.Exp, bias=minus_max, accum_out=total)
 
         def normalise(b):
-            total, inverse = stats[b][:, 8:9], stats[b][:, 16:17]
+            total, inverse = stats[b][:, 1, 0:1], stats[b][:, 2, 0:1]
             nc.vector.reciprocal(out=inverse, in_=total)
-            normed = keep.tile([P, PACK, P], F32, name="normed%d" % b)
+            shares = keep.tile([P, PACK, P], F32, name="shares%d" % b)
             if b == 2:
-                nc.scalar.activation(out=normed[:], in_=shares[b][:], func=ACT.Copy, scale=inverse)
+                nc.scalar.activation(out=shares[:], in_=powers[b][:], func=ACT.Copy, scale=inverse)
             else:
-                nc.vector.tensor_scalar(out=normed[:], in0=shares[b][:], scalar1=inverse, scalar2=None, op0=ALU.mult)
-            turn(b, normed, False)
-
-        errors = [keep.tile([P, P, PACK], BF16, name="errors%d" % b, align_bytes=64) for b in range(BLOCKS)]
+                nc.vector.tensor_scalar(out=shares[:], in0=powers[b][:], scalar1=inverse, scalar2=None, op0=ALU.mult)
+            turn(b, shares, False)
 
         def weigh(b):
             nc.vector.tensor_tensor(out=errors[b][:], in0=turned[b][:].rearrange("p r t -> p t r"),
                                     in1=factors[:].unsqueeze(1).to_broadcast([P, P, PACK]), op=ALU.mult)
 
         def quantise(b):
-            cols = slice(pad + b * P, pad + (b + 1) * P)
-            nc.vector.quantize_mx(out=codes[:, cols].bitcast(E5M2), scales=plane[:, cols], in_=errors[b][:].rearrange("p t r -> p (t r)"))
+            columns = slice(PAD + b * P, PAD + (b + 1) * P)
+            nc.vector.quantize_mx(out=codes[:, columns].bitcast(E5M2), scales=plane[:, columns], in_=errors[b][:].rearrange("p t r -> p (t r)"))
 
-        def product(b, first_column, skip, bank, copy):
-            rows = slice(b * P, (b + 1) * P)
+        def product(rows_block, first_column, skip, bank, copy):
+            rows = slice(rows_block * P, (rows_block + 1) * P)
             window = slice(first_column, first_column + T)
             acc = psum.tile([P, T], F32, name="acc", tag=bank)
             nc.tensor.matmul_mx(out=acc[:], lhsT=fixed_words[:, rows].bitcast(E4M3), lhsT_scale=fixed_plane[:, rows],
                                 rhs=codes[:, window].bitcast(E5M2), rhs_scale=plane[:, window], start=True, stop=True)
             result = keep.tile([P, T - skip], F32, name="result", tag="result_" + bank)
             copy(out=result[:], in_=acc[:, skip:])
-            first_token = first_column + skip - pad
+            first_token = first_column + skip - PAD
             nc.sync.dma_start(out=out[rows, first_token : first_token + T - skip], in_=result[:])
 
         exponentiate(0)
@@ -158,11 +164,11 @@ def tile_list_class_error_back_kernel(tc, xt_words, xt_scales, wc_words, wc_scal
         weigh(2)
         quantise(1)
         weigh(3)
-        product(0, 0, pad, "bank0", nc.scalar.copy)
-        product(1, 0, pad, "bank1", nc.scalar.copy)
+        product(0, 0, PAD, "bank0", nc.scalar.copy)
+        product(1, 0, PAD, "bank1", nc.scalar.copy)
         quantise(2)
         quantise(3)
-        product(2, pad, 0, "bank2", nc.scalar.copy)
-        product(3, pad, 0, "bank3", nc.vector.tensor_copy)
-        product(0, pad, pad, "turned0", nc.scalar.copy)
-        product(1, pad, pad, "turned1", nc.vector.tensor_copy)
+        product(2, PAD, 0, "bank2", nc.scalar.copy)
+        product(3, PAD, 0, "bank3", nc.vector.tensor_copy)
+        product(0, PAD, T // 2, "turned0", nc.scalar.copy)
+        product(1, PAD, T // 2, "turned1", nc.vector.tensor_copy)

from contextlib import ExitStack

import concourse.mybir as mybir

K, T, C, J, N = 512, 512, 2048, 512, 512
FLOPS = 2 * K * T * J + 2 * J * N * T

F32 = mybir.dt.float32
BF16 = mybir.dt.bfloat16
I32 = mybir.dt.int32
U32 = mybir.dt.uint32
U16 = mybir.dt.uint16
U8 = mybir.dt.uint8
E4M3 = mybir.dt.float8_e4m3fn_x4
E5M2 = mybir.dt.float8_e5m2_x4
E2M1 = mybir.dt.float4_e2m1fn_x4
ACT = mybir.ActivationFunctionType
ALU = mybir.AluOpType
AX = mybir.AxisListType

P = 128
PACK = 4
QUADRANT = 32
LIST_ROWS = 16
BLOCKS = T // P
PAD = T // 2
PAIR_BYTES = 2 * J * 4


def load_plane(nc, plane, rows):
    for quad in range(P // QUADRANT):
        first = QUADRANT * quad
        nc.sync.dma_start(out=plane[first : first + PACK, :].bitcast(I32), in_=rows[0, PACK * quad : PACK * (quad + 1), :].bitcast(I32))


def load_words(nc, words, packed):
    nc.sync.dma_start(out=words[:].bitcast(I32), in_=packed[0].rearrange("p n r -> p (n r)").bitcast(I32))


def tile_list_class_error_back_kernel(tc, xt_words, xt_scales, wc_words, wc_scales, tg, fj, wo_words, wo_scales, offs, out):
    nc = tc.nc
    with ExitStack() as ctx:
        keep = ctx.enter_context(tc.tile_pool(name="keep", bufs=1))
        reused = ctx.enter_context(tc.tile_pool(name="reused", bufs=1))
        psum = ctx.enter_context(tc.psum_pool(name="psum", bufs=1))

        offsets = keep.tile([P, J // LIST_ROWS], U16, name="offsets")
        nc.sync.dma_start(offsets[:], offs)
        factors = keep.tile([P, PACK], F32, name="factors")
        nc.sync.dma_start(out=factors[:], in_=fj.rearrange("(p r) o -> p (r o)", r=PACK))

        wc_plane = keep.tile([P, C], U8, name="wc_plane", align_bytes=64)
        nc.vector.memset(wc_plane[:].bitcast(I32), 0)
        load_plane(nc, wc_plane, wc_scales)
        wc_table = keep.tile([P, C], U16, name="wc_table", align_bytes=64)
        nc.sync.dma_start(out=wc_table[:].bitcast(I32), in_=wc_words[0].bitcast(I32))

        fixed_words = keep.tile([P, T], U32, name="fixed_words", align_bytes=64)
        load_words(nc, fixed_words, xt_words)
        fixed_plane = keep.tile([P, T], U8, name="fixed_plane", align_bytes=64)
        nc.vector.memset(fixed_plane[:].bitcast(I32), 0)
        load_plane(nc, fixed_plane, xt_scales)

        ones = keep.tile([P, P], F32, name="ones")
        nc.vector.memset(ones[:], 1.0)
        ident = keep.tile([P, P], F32, name="ident")
        nc.gpsimd.affine_select(out=ident[:], in_=ones[:], compare_op=ALU.is_equal, fill=0.0, base=0, pattern=[[-1, P]], channel_multiplier=1)

        warm = keep.tile([P, 16], F32, name="warm")
        nc.scalar.activation(out=warm[:], in_=ones[:, 0:16], func=ACT.Exp)

        targets = [reused.tile([P, 2, J], F32, name="targets%d" % pair, offset=pair * PAIR_BYTES) for pair in range(BLOCKS // 2)]
        for b in range(BLOCKS):
            nc.sync.dma_start(out=targets[b // 2][:, b % 2, :], in_=tg[b * P : (b + 1) * P, :])

        picked_plane = keep.tile([P, J], U8, name="picked_plane", align_bytes=64)
        picked_words = keep.tile([P, J], U16, name="picked_words", align_bytes=64)
        halves = [slice(h * J // 2, (h + 1) * J // 2) for h in range(2)]
        nc.vector.tensor_copy(picked_plane[:], wc_plane[:].indirect(offsets[:]))
        for half in halves:
            nc.vector.tensor_copy(picked_words[:, half], wc_table[:].indirect(offsets[:, half.start // LIST_ROWS : half.stop // LIST_ROWS]))

        logits = [psum.tile([P, J], F32, name="logits%d" % b, tag="bank%d" % b) for b in range(BLOCKS)]
        passes = [(b, half) for half in halves for b in range(2)] + [(b, slice(0, J)) for b in range(2, BLOCKS)]
        for b, classes in passes:
            tokens = slice(b * P, (b + 1) * P)
            nc.tensor.matmul_mx(out=logits[b][:, classes], lhsT=fixed_words[:, tokens].bitcast(E4M3), lhsT_scale=fixed_plane[:, tokens],
                                rhs=picked_words[:, classes].bitcast(E2M1), rhs_scale=picked_plane[:, classes], start=True, stop=True)

        load_words(nc, fixed_words, wo_words)
        load_plane(nc, fixed_plane, wo_scales)

        turned = [psum.tile([P, PACK, P], F32, name="turned%d" % b) for b in range(BLOCKS)]

        def turn(b, src, opens):
            for r in range(PACK):
                nc.tensor.matmul(turned[b][:, r, :], src[:, r, :], ident[:], start=opens and r == 0, stop=(not opens) and r == PACK - 1, is_transpose=True)

        for b in range(BLOCKS):
            src = targets[b // 2][:, b % 2, :]
            minus_tg = keep.tile([P, PACK, P], F32, name="minus_tg%d" % b)
            if b < 2:
                nc.scalar.activation(out=minus_tg[:].rearrange("p r q -> p q r"), in_=src.rearrange("p (q r) -> p q r", r=PACK), func=ACT.Copy, scale=-1.0)
            else:
                nc.gpsimd.tensor_scalar(out=minus_tg[:].rearrange("p r (g q) -> p g r q", q=PACK), in0=src.rearrange("p (g q r) -> p g r q", q=PACK, r=PACK),
                                        scalar1=-1.0, scalar2=1.0, op0=ALU.mult, op1=ALU.mult)
            turn(b, minus_tg, True)

        codes = keep.tile([P, PAD + T], U32, name="codes", align_bytes=64)
        plane = keep.tile([P, PAD + T], U8, name="plane", align_bytes=64)
        nc.vector.memset(codes[:, :PAD].bitcast(I32), 0)
        nc.vector.memset(plane[:, :PAD].bitcast(I32), 0)

        stats = [keep.tile([P, 3, 8], F32, name="stats%d" % b) for b in range(BLOCKS)]
        powers = [reused.tile([P, PACK, P], F32, name="powers0", offset=0)]
        powers.extend(keep.tile([P, PACK, P], F32, name="powers%d" % b) for b in range(1, BLOCKS))
        errors = [keep.tile([P, P, PACK], BF16, name="errors%d" % b, align_bytes=64) for b in range(BLOCKS)]

        def exponentiate(b):
            minus_max, total = stats[b][:, 0, 0:1], stats[b][:, 1, 0:1]
            nc.vector.tensor_reduce(out=minus_max, in_=logits[b][:], axis=AX.X, op=ALU.max, negate=True)
            nc.scalar.activation(out=powers[b][:], in_=logits[b][:].rearrange("p (q r) -> p r q", r=PACK), func=ACT.Exp, bias=minus_max, accum_out=total)

        def normalise(b):
            total, inverse = stats[b][:, 1, 0:1], stats[b][:, 2, 0:1]
            nc.vector.reciprocal(out=inverse, in_=total)
            shares = keep.tile([P, PACK, P], F32, name="shares%d" % b)
            if b == 2:
                nc.scalar.activation(out=shares[:], in_=powers[b][:], func=ACT.Copy, scale=inverse)
            else:
                nc.vector.tensor_scalar(out=shares[:], in0=powers[b][:], scalar1=inverse, scalar2=None, op0=ALU.mult)
            turn(b, shares, False)

        def weigh(b):
            nc.vector.tensor_tensor(out=errors[b][:], in0=turned[b][:].rearrange("p r t -> p t r"),
                                    in1=factors[:].unsqueeze(1).to_broadcast([P, P, PACK]), op=ALU.mult)

        def quantise(b):
            columns = slice(PAD + b * P, PAD + (b + 1) * P)
            nc.vector.quantize_mx(out=codes[:, columns].bitcast(E5M2), scales=plane[:, columns], in_=errors[b][:].rearrange("p t r -> p (t r)"))

        def product(rows_block, first_column, skip, bank, copy):
            rows = slice(rows_block * P, (rows_block + 1) * P)
            window = slice(first_column, first_column + T)
            acc = psum.tile([P, T], F32, name="acc", tag=bank)
            nc.tensor.matmul_mx(out=acc[:], lhsT=fixed_words[:, rows].bitcast(E4M3), lhsT_scale=fixed_plane[:, rows],
                                rhs=codes[:, window].bitcast(E5M2), rhs_scale=plane[:, window], start=True, stop=True)
            result = keep.tile([P, T - skip], F32, name="result", tag="result_" + bank)
            copy(out=result[:], in_=acc[:, skip:])
            first_token = first_column + skip - PAD
            nc.sync.dma_start(out=out[rows, first_token : first_token + T - skip], in_=result[:])

        exponentiate(0)
        exponentiate(1)
        normalise(0)
        exponentiate(2)
        normalise(1)
        exponentiate(3)
        weigh(0)
        normalise(2)
        normalise(3)
        weigh(1)
        quantise(0)
        weigh(2)
        quantise(1)
        weigh(3)
        product(0, 0, PAD, "bank0", nc.scalar.copy)
        product(1, 0, PAD, "bank1", nc.scalar.copy)
        quantise(2)
        quantise(3)
        product(2, PAD, 0, "bank2", nc.scalar.copy)
        product(3, PAD, 0, "bank3", nc.vector.tensor_copy)
        product(0, PAD, T // 2, "turned0", nc.scalar.copy)
        product(1, PAD, T // 2, "turned1", nc.vector.tensor_copy)
